import numpy as np
import ml_dtypes


def mxq(x, axis, fmt="e4m3"):
    dtype, down = {"e4m3": (ml_dtypes.float8_e4m3fn, 7), "e5m2": (ml_dtypes.float8_e5m2, 14)}[fmt]
    v = np.moveaxis(np.asarray(x, np.float32).astype(ml_dtypes.bfloat16).astype(np.float64), axis, -1)
    blocks = v.reshape(v.shape[:-1] + (-1, 32))
    amax = np.abs(blocks).max(-1, keepdims=True)
    byte = np.maximum(np.where(amax > 0, np.frexp(amax)[1] - 1 + 127, 0) - down, 1)
    scale = np.exp2(byte - 127.0)
    codes = (blocks / scale).astype(np.float32).astype(dtype).astype(np.float64)
    return np.moveaxis((codes * scale).reshape(v.shape), -1, axis)


WIDE = False


def mx_kscale(k):
    if not WIDE:
        return np.ones(k)
    levels = np.array([10, -10, 5, -5, 0])
    if k % 512:
        return np.exp2(np.random.permutation(np.resize(levels, k // 32))).repeat(32)
    a = np.empty((k // 512, 16))
    for p in range(k // 512):
        a[p, :8] = np.random.permutation(np.resize(levels, 8))
        for g in range(8):
            far = levels[np.abs(levels - a[p, g]) >= 10]
            a[p, g + 8] = far[np.random.randint(len(far))]
    return np.exp2(a.ravel()).repeat(32)


def f64(x):
    return np.asarray(x).astype(np.float64)


def striped(idx):
    return np.tile(idx.reshape(-1, 16).T, (8, 1)).astype(np.uint16)


def unstriped(offs):
    return offs[:16].T.reshape(-1).astype(np.int64)


E2M1 = np.array([0.0, 0.5, 1.0, 1.5, 2.0, 3.0, 4.0, 6.0, -0.0, -0.5, -1.0, -1.5, -2.0, -3.0, -4.0, -6.0])


def pack_weight(w, fmt):
    k, n = w.shape
    w = f64(np.asarray(w, np.float32).astype(ml_dtypes.bfloat16)).reshape(k // 32, 32, n)
    amax = np.abs(w).max(1)
    if fmt == "e4m3":
        byte = np.frexp(amax)[1] - 1 + 127 - 7
    else:
        mant, ex = np.frexp(amax / 6.0)
        byte = np.where(mant > 0.5, ex, ex - 1) + 127
    byte = np.clip(np.where(amax > 0, byte, 1), 1, 254)
    scaled = (w * np.exp2(127.0 - byte)[:, None, :]).reshape(k, n).astype(np.float32)
    by_word = np.ascontiguousarray(scaled.reshape(k // 512, 128, 4, n).transpose(0, 1, 3, 2))
    if fmt == "e4m3":
        words = by_word.astype(ml_dtypes.float8_e4m3fn).view(np.uint8)
    else:
        c = by_word.astype(ml_dtypes.float4_e2m1fn).view(np.uint8) & 0xF
        words = (c[..., 0::2] | (c[..., 1::2] << 4)).reshape(k // 512, 128, 2 * n)
    return np.ascontiguousarray(words), np.ascontiguousarray(byte.astype(np.uint8).reshape(k // 512, 16, n))


def unpack_weight(words, scales, fmt):
    g, _, n = scales.shape
    words = np.ascontiguousarray(words).reshape(g, 128, n, -1)
    if fmt == "e4m3":
        vals = words.view(ml_dtypes.float8_e4m3fn).astype(np.float64)
    else:
        nib = np.empty((g, 128, n, 4), np.uint8)
        nib[..., 0::2] = words & 0xF
        nib[..., 1::2] = words >> 4
        vals = E2M1[nib]
    vals = vals * np.repeat(np.exp2(scales.astype(np.float64) - 127.0), 8, axis=1)[..., None]
    return vals.transpose(0, 1, 3, 2).reshape(g * 512, n)


K, T, E, C, N = 256, 1024, 16, 256, 512
TOP = 4


def by_expert(wq, xq):
    return np.concatenate([wq[e].T @ xq[:, e * C:(e + 1) * C] for e in range(E)], axis=1)


def setup_inputs():
    n = np.random.standard_normal
    s = mx_kscale(N)[:, None]
    deal = np.repeat(np.arange(E), C).reshape(TOP, T)[:, np.random.permutation(T)]
    deal = np.take_along_axis(deal, np.argsort(np.random.rand(TOP, T), axis=0), axis=0)
    for _ in range(8):
        s_, t_ = np.random.permutation(T).reshape(2, -1); r = np.random.randint(TOP, size=T // 2); x, y = deal[r, s_].copy(), deal[r, t_].copy()
        ok = ~((deal[:, s_] == y).any(0) | (deal[:, t_] == x).any(0)); deal[r[ok], s_[ok]] = y[ok]; deal[r[ok], t_[ok]] = x[ok]
    order = np.lexsort((np.random.rand(TOP * T), deal.reshape(-1)))
    slot_token = order % T; pos = np.empty(TOP * T, np.int64); pos[order] = np.arange(TOP * T); pos = pos.reshape(TOP, T)
    g = np.random.uniform(0.5, 1.5, (TOP, T)); g = g / g.sum(0)
    w_slot = np.empty(E * C)
    for r in range(TOP): w_slot[pos[r]] = g[r]
    w = [pack_weight(m, "e2m1") for m in n((E + 1, N, K)) / np.sqrt(N) / s[None]]
    return {
        "dyT": (n((N, T)) * s).astype(np.float32),
        "w_words": np.stack([m[0] for m in w]),
        "w_scales": np.stack([m[1] for m in w]),
        "gate": np.tile(w_slot, (N, 1)).astype(np.float32),
        "offs": striped(slot_token),
        "pos1": striped(pos[0]),
        "pos2": striped(pos[1]),
        "pos3": striped(pos[2]),
        "pos4": striped(pos[3]),
    }


def reference(dyT, w_words, w_scales, gate, offs, pos1, pos2, pos3, pos4):
    idx = unstriped(offs)
    w = np.stack([unpack_weight(w_words[e], w_scales[e], "e2m1") for e in range(E + 1)])
    gq = mxq(f64(gate) * f64(dyT)[:, idx], 0, "e4m3")
    wq = w
    ds = wq[E].T @ mxq(f64(dyT), 0, "e4m3")
    dx = by_expert(wq, gq)
    return ds + dx[:, unstriped(pos1)] + dx[:, unstriped(pos2)] + dx[:, unstriped(pos3)] + dx[:, unstriped(pos4)]

@@ -1,0 +1,216 @@
+from contextlib import ExitStack
+
+import concourse.mybir as mybir
+from concourse.masks import make_identity
+
+K, T, E, C, N = 256, 1024, 16, 256, 512
+TOP = 4
+S = E * C
+FLOPS = 2 * N * K * (S + T)
+
+F32 = mybir.dt.float32
+BF16 = mybir.dt.bfloat16
+I32 = mybir.dt.int32
+U32 = mybir.dt.uint32
+U16 = mybir.dt.uint16
+U8 = mybir.dt.uint8
+FP8X4 = mybir.dt.float8_e4m3fn_x4
+FP4X4 = mybir.dt.float4_e2m1fn_x4
+MULT = mybir.AluOpType.mult
+ADD = mybir.AluOpType.add
+
+P = 128
+PACK = 4
+BANK = 512
+STRIPE = 16
+CHUNKS = [512] * 7 + [256, 128, 128]
+HEAD = 2
+SHARED_PIECE = 256
+
+
+def tile_moe_bds_lin_none_kernel(
+    tc, dyT, w_words, w_scales, gate, offs, pos1, pos2, pos3, pos4, out
+):
+    nc = tc.nc
+    starts = [sum(CHUNKS[:c]) for c in range(len(CHUNKS))]
+    dy_rows = dyT.rearrange("(p j) t -> p j t", j=PACK)
+    gate_rows = gate.rearrange("(p j) s -> p j s", j=PACK)
+
+    with ExitStack() as ctx:
+        lists = ctx.enter_context(tc.tile_pool(name="lists", bufs=1))
+        keep = ctx.enter_context(tc.tile_pool(name="keep", bufs=1))
+        ring = ctx.enter_context(tc.tile_pool(name="ring", bufs=3))
+        psum = ctx.enter_context(tc.psum_pool(name="psum", bufs=2))
+
+        offs_sb = lists.tile([P, S // STRIPE], U16, name="offs_sb")
+        pos_sb = [lists.tile([P, T // STRIPE], U16, name=f"pos_sb{r}") for r in range(TOP)]
+        window = [keep.tile([P, T], F32, name=f"window{j}") for j in range(PACK)]
+        words = keep.tile([P, E + 1, 2 * K], U8, name="words", align_bytes=64)
+        wscale = keep.tile([P, E + 1, K], U8, name="wscale", align_bytes=64)
+        dx = [keep.tile([P, S], F32, name=f"dx{m}") for m in range(K // P)]
+        ds = [keep.tile([P, T], F32, name=f"ds{m}") for m in range(K // P)]
+        ident = keep.tile([P, P], F32, name="ident")
+
+        nc.gpsimd.memset(wscale[:].rearrange("p e k -> p (e k)").bitcast(I32), 0)
+        make_identity(nc, ident[:])
+
+        def stream_tile(width):
+            return ring.tile([P, PACK, width], F32, name="stream", tag="stream", bufs=7)
+
+        def load_gate(c):
+            t = stream_tile(CHUNKS[c])
+            nc.sync.dma_start(out=t[:], in_=gate_rows[:, :, starts[c] : starts[c] + CHUNKS[c]])
+            return t
+
+        def load_words(e0, e1):
+            nc.sync.dma_start(
+                out=words[:, e0:e1, :].bitcast(I32),
+                in_=w_words[e0:e1, 0].rearrange("e p b -> p e b").bitcast(I32),
+            )
+
+        nc.sync.dma_start(offs_sb[:], offs)
+        gates = [stream_tile(CHUNKS[c]) for c in range(HEAD)]
+        for j in range(PACK):
+            nc.sync.dma_start(out=window[j][:], in_=dy_rows[:, j, :])
+            for c in range(HEAD):
+                nc.sync.dma_start(
+                    out=gates[c][:, j, :], in_=gate_rows[:, j, starts[c] : starts[c] + CHUNKS[c]]
+                )
+        gates.append(load_gate(2))
+        for q in range(4):
+            nc.sync.dma_start(
+                out=wscale[32 * q : 32 * q + 4, :, :].bitcast(I32),
+                in_=w_scales[:, 0, 4 * q : 4 * q + 4, :].rearrange("e f k -> f e k").bitcast(I32),
+            )
+        load_words(0, 6)
+        gates.append(load_gate(3))
+        load_words(6, E + 1)
+        gates.append(load_gate(4))
+        dy_again = []
+        for h in range(T // BANK):
+            t = stream_tile(BANK)
+            nc.sync.dma_start(out=t[:], in_=dy_rows[:, :, h * BANK : (h + 1) * BANK])
+            dy_again.append(t)
+        for r, pos in enumerate((pos1, pos2, pos3, pos4)):
+            nc.sync.dma_start(pos_sb[r][:], pos)
+        for c in range(5, len(CHUNKS)):
+            gates.append(load_gate(c))
+
+        def gather_plane(c, g, j):
+            cols = slice(starts[c] // STRIPE, (starts[c] + CHUNKS[c]) // STRIPE)
+            nc.vector.tensor_tensor(
+                g[:, j, :], window[j][:].indirect(offs_sb[:, cols]), gates[c][:, j, :], MULT
+            )
+
+        def product_tile(c):
+            return ring.tile([P, PACK, CHUNKS[c]], F32, name="product", tag="product", bufs=4)
+
+        def interleave(dst, src):
+            nc.scalar.copy(
+                out=dst.rearrange("p (c i) j -> p c j i", i=4),
+                in_=src.rearrange("p j (c i) -> p c j i", i=4),
+            )
+
+        def quantize(grouped, width):
+            codes = ring.tile([P, width], U32, name="codes", tag="codes", align_bytes=64)
+            scales = ring.tile([P, width], U8, name="scales", tag="scales", align_bytes=64)
+            nc.vector.quantize_mx(
+                out=codes[:].bitcast(FP8X4),
+                scales=scales[:],
+                in_=grouped[:].rearrange("p c j -> p (c j)"),
+            )
+            return codes, scales
+
+        def multiply(codes, scales, pieces, targets):
+            width = sum(n for e, n in pieces)
+            for m in range(K // P):
+                bank = psum.tile([P, BANK], F32, name="mx_bank", tag="mx_bank", bufs=4)
+                at = 0
+                for e, n in pieces:
+                    nc.tensor.matmul_mx(
+                        out=bank[:, at : at + n],
+                        lhsT=words[:, e, 2 * P * m : 2 * P * (m + 1)].bitcast(FP4X4),
+                        lhsT_scale=wscale[:, e, P * m : P * (m + 1)],
+                        rhs=codes[:, at : at + n].bitcast(FP8X4),
+                        rhs_scale=scales[:, at : at + n],
+                        start=True,
+                        stop=True,
+                    )
+                    at += n
+                nc.scalar.copy(out=targets[m], in_=bank[:, :width])
+
+        def finish_chunk(c, g):
+            width = CHUNKS[c]
+            grouped = ring.tile([P, width, PACK], BF16, name="grouped", tag="grouped", align_bytes=64)
+            interleave(grouped[:], g[:])
+            codes, scales = quantize(grouped, width)
+            n = min(width, C)
+            pieces = [((starts[c] + a) // C, n) for a in range(0, width, n)]
+            multiply(codes, scales, pieces, [d[:, starts[c] : starts[c] + width] for d in dx])
+
+        products = [product_tile(c) for c in range(HEAD)]
+        for j in range(PACK):
+            for c in range(HEAD):
+                gather_plane(c, products[c], j)
+        for c in range(len(CHUNKS)):
+            ahead = c + 1
+            if HEAD <= ahead < len(CHUNKS):
+                products.append(product_tile(ahead))
+                for j in range(PACK):
+                    gather_plane(ahead, products[ahead], j)
+            finish_chunk(c, products[c])
+
+        for h in range(T // BANK):
+            grouped = keep.tile([P, BANK, PACK], BF16, name=f"shared{h}", align_bytes=64)
+            for a in range(0, BANK, SHARED_PIECE):
+                interleave(grouped[:, a : a + SHARED_PIECE, :], dy_again[h][:, :, a : a + SHARED_PIECE])
+            codes, scales = quantize(grouped, BANK)
+            multiply(codes, scales, [(E, BANK)], [d[:, h * BANK : (h + 1) * BANK] for d in ds])
+
+        def fetch(m, h, r):
+            got = ring.tile([P, BANK], F32, name="got", tag="got", bufs=8)
+            cols = slice(h * BANK // STRIPE, (h + 1) * BANK // STRIPE)
+            nc.vector.tensor_copy(got[:], dx[m][:].indirect(pos_sb[r][:, cols]))
+            return got
+
+        def add_turned(bank, term, first, last):
+            for b in range(BANK // P):
+                nc.tensor.matmul(
+                    bank[:, b * P : (b + 1) * P],
+                    term[:, b * P : (b + 1) * P],
+                    ident[:],
+                    start=first and b == 0,
+                    stop=last and b == BANK // P - 1,
+                    is_transpose=True,
+                )
+
+        def sum_terms(m, h, count):
+            bank = psum.tile([P, BANK], F32, name="sum_bank", tag="sum_bank")
+            add_turned(bank, ds[m][:, h * BANK : (h + 1) * BANK], True, False)
+            for r in range(count):
+                add_turned(bank, fetch(m, h, r), False, r == count - 1)
+            turned = ring.tile([P, BANK], F32, name="turned", tag="turned")
+            nc.scalar.copy(out=turned[:], in_=bank[:])
+            back = psum.tile([P, BANK], F32, name="back_bank", tag="back_bank")
+            for b in range(BANK // P):
+                nc.tensor.transpose(back[:, b * P : (b + 1) * P], turned[:, b * P : (b + 1) * P], ident[:])
+            return back
+
+        def store(m, h, result):
+            nc.sync.dma_start(out=out[m * P : (m + 1) * P, h * BANK : (h + 1) * BANK], in_=result[:])
+
+        def result_tile():
+            return ring.tile([P, BANK], F32, name="result", tag="result", bufs=4)
+
+        halves = range(T // BANK)
+        for h in halves:
+            back = sum_terms(0, h, TOP)
+            result = result_tile()
+            nc.scalar.copy(out=result[:], in_=back[:])
+            store(0, h, result)
+        backs = [sum_terms(1, h, TOP - 1) for h in halves]
+        lasts = [fetch(1, h, TOP - 1) for h in halves]
+        for h in halves:
+            result = result_tile()
+            nc.vector.tensor_tensor(result[:], backs[h][:], lasts[h][:], ADD)
+            store(1, h, result)

@@ -25,7 +25,11 @@ BANK = 512
 STRIPE = 16
 CHUNKS = [512] * 7 + [256, 128, 128]
 HEAD = 2
-SHARED_PIECE = 256
+GATE_SLOT = ["gate0", "gate1", "gate2", "gate3", "gate4", "gate0", "gate1", "gate7", "gate8"]
+PRODUCT_SLOT = ["a", "b", "c", "a", "b", "d", "a", "b", "gate7", "c"]
+GROUPED_SLOT = ["e", "a", "b", "d", "a", "b", "c", "a", "e", "b"]
+CODES_SLOT = ["gate2", "d", "gate3", "gate4", "gate0", "gate1", "gate8", None, None, None]
+SHARED_PIECE = 128
 
 
 def tile_moe_bds_lin_none_kernel(
@@ -33,6 +37,7 @@ def tile_moe_bds_lin_none_kernel(
 ):
     nc = tc.nc
     starts = [sum(CHUNKS[:c]) for c in range(len(CHUNKS))]
+    last = len(CHUNKS) - 1
     dy_rows = dyT.rearrange("(p j) t -> p j t", j=PACK)
     gate_rows = gate.rearrange("(p j) s -> p j s", j=PACK)
 
@@ -54,13 +59,18 @@ def tile_moe_bds_lin_none_kernel(
         nc.gpsimd.memset(wscale[:].rearrange("p e k -> p (e k)").bitcast(I32), 0)
         make_identity(nc, ident[:])
 
-        def stream_tile(width):
-            return ring.tile([P, PACK, width], F32, name="stream", tag="stream", bufs=7)
+        def slot_tile(slot, shape, dtype):
+            return keep.tile(shape, dtype, name=slot, tag=slot, align_bytes=64)
 
-        def load_gate(c):
-            t = stream_tile(CHUNKS[c])
-            nc.sync.dma_start(out=t[:], in_=gate_rows[:, :, starts[c] : starts[c] + CHUNKS[c]])
-            return t
+        def load_gate(c, slot, j0, j1, by_plane=False):
+            t = slot_tile(slot, [P, j1 - j0, CHUNKS[c]], F32)
+            src = gate_rows[:, j0:j1, starts[c] : starts[c] + CHUNKS[c]]
+            if by_plane:
+                for j in range(j1 - j0):
+                    nc.sync.dma_start(out=t[:, j, :], in_=src[:, j, :])
+            else:
+                nc.sync.dma_start(out=t[:], in_=src)
+            return [t[:, j, :] for j in range(j1 - j0)]
 
         def load_words(e0, e1):
             nc.sync.dma_start(
@@ -69,51 +79,54 @@ def tile_moe_bds_lin_none_kernel(
             )
 
         nc.sync.dma_start(offs_sb[:], offs)
-        gates = [stream_tile(CHUNKS[c]) for c in range(HEAD)]
+        head = [slot_tile(GATE_SLOT[c], [P, PACK, CHUNKS[c]], F32) for c in range(HEAD)]
         for j in range(PACK):
             nc.sync.dma_start(out=window[j][:], in_=dy_rows[:, j, :])
             for c in range(HEAD):
                 nc.sync.dma_start(
-                    out=gates[c][:, j, :], in_=gate_rows[:, j, starts[c] : starts[c] + CHUNKS[c]]
+                    out=head[c][:, j, :], in_=gate_rows[:, j, starts[c] : starts[c] + CHUNKS[c]]
                 )
-        gates.append(load_gate(2))
-        for q in range(4):
+        gates = [[t[:, j, :] for j in range(PACK)] for t in head]
+        gates.append(load_gate(2, GATE_SLOT[2], 0, PACK, True))
+        gates.append(load_gate(3, GATE_SLOT[3], 0, PACK))
+        for q in (0, 2, 1, 3):
             nc.sync.dma_start(
                 out=wscale[32 * q : 32 * q + 4, :, :].bitcast(I32),
                 in_=w_scales[:, 0, 4 * q : 4 * q + 4, :].rearrange("e f k -> f e k").bitcast(I32),
             )
         load_words(0, 6)
-        gates.append(load_gate(3))
+        gates.append(load_gate(4, GATE_SLOT[4], 0, PACK))
         load_words(6, E + 1)
-        gates.append(load_gate(4))
-        dy_again = []
-        for h in range(T // BANK):
-            t = stream_tile(BANK)
-            nc.sync.dma_start(out=t[:], in_=dy_rows[:, :, h * BANK : (h + 1) * BANK])
-            dy_again.append(t)
+        for c in range(5, last):
+            gates.append(load_gate(c, GATE_SLOT[c], 0, PACK))
+        gates.append(load_gate(last, "gate9a", 0, PACK - 1) + load_gate(last, "gate9b", PACK - 1, PACK))
         for r, pos in enumerate((pos1, pos2, pos3, pos4)):
             nc.sync.dma_start(pos_sb[r][:], pos)
-        for c in range(5, len(CHUNKS)):
-            gates.append(load_gate(c))
+
+        rounded = keep.tile([P, PACK, BANK], BF16, name="rounded")
+        shared1 = keep.tile([P, BANK, PACK], BF16, name="shared1", align_bytes=64)
+        for j in range(PACK):
+            nc.scalar.copy(out=rounded[:, j, :], in_=window[j][:, :BANK])
+            nc.scalar.copy(out=shared1[:, :, j], in_=window[j][:, BANK:])
 
         def gather_plane(c, g, j):
             cols = slice(starts[c] // STRIPE, (starts[c] + CHUNKS[c]) // STRIPE)
             nc.vector.tensor_tensor(
-                g[:, j, :], window[j][:].indirect(offs_sb[:, cols]), gates[c][:, j, :], MULT
+                g[:, j, :], window[j][:].indirect(offs_sb[:, cols]), gates[c][j], MULT
             )
 
-        def product_tile(c):
-            return ring.tile([P, PACK, CHUNKS[c]], F32, name="product", tag="product", bufs=4)
-
-        def interleave(dst, src):
-            nc.scalar.copy(
+        def interleave(copy, dst, src):
+            copy(
                 out=dst.rearrange("p (c i) j -> p c j i", i=4),
                 in_=src.rearrange("p j (c i) -> p c j i", i=4),
             )
 
-        def quantize(grouped, width):
-            codes = ring.tile([P, width], U32, name="codes", tag="codes", align_bytes=64)
-            scales = ring.tile([P, width], U8, name="scales", tag="scales", align_bytes=64)
+        def quantize(grouped, width, slot=None):
+            if slot:
+                codes = slot_tile(slot, [P, width], U32)
+            else:
+                codes = ring.tile([P, width], U32, name="codes", tag="codes", bufs=4, align_bytes=64)
+            scales = ring.tile([P, width], U8, name="scales", tag="scales", bufs=7, align_bytes=64)
             nc.vector.quantize_mx(
                 out=codes[:].bitcast(FP8X4),
                 scales=scales[:],
@@ -121,54 +134,97 @@ def tile_moe_bds_lin_none_kernel(
             )
             return codes, scales
 
-        def multiply(codes, scales, pieces, targets):
-            width = sum(n for e, n in pieces)
-            for m in range(K // P):
-                bank = psum.tile([P, BANK], F32, name="mx_bank", tag="mx_bank", bufs=4)
-                at = 0
-                for e, n in pieces:
-                    nc.tensor.matmul_mx(
-                        out=bank[:, at : at + n],
-                        lhsT=words[:, e, 2 * P * m : 2 * P * (m + 1)].bitcast(FP4X4),
-                        lhsT_scale=wscale[:, e, P * m : P * (m + 1)],
-                        rhs=codes[:, at : at + n].bitcast(FP8X4),
-                        rhs_scale=scales[:, at : at + n],
-                        start=True,
-                        stop=True,
-                    )
-                    at += n
-                nc.scalar.copy(out=targets[m], in_=bank[:, :width])
+        def mx_bank():
+            return psum.tile([P, BANK], F32, name="mx_bank", tag="mx_bank", bufs=4)
 
-        def finish_chunk(c, g):
+        def multiply(bank, m, codes, scales, pieces):
+            at = 0
+            for e, n in pieces:
+                nc.tensor.matmul_mx(
+                    out=bank[:, at : at + n],
+                    lhsT=words[:, e, 2 * P * m : 2 * P * (m + 1)].bitcast(FP4X4),
+                    lhsT_scale=wscale[:, e, P * m : P * (m + 1)],
+                    rhs=codes[:, at : at + n].bitcast(FP8X4),
+                    rhs_scale=scales[:, at : at + n],
+                    start=True,
+                    stop=True,
+                )
+                at += n
+
+        products, grouped, quantized = {}, {}, {}
+
+        def gather(chunks):
+            for c in chunks:
+                products[c] = slot_tile(PRODUCT_SLOT[c], [P, PACK, CHUNKS[c]], F32)
+            for j in range(PACK):
+                for c in chunks:
+                    gather_plane(c, products[c], j)
+
+        def group(c):
+            grouped[c] = slot_tile(GROUPED_SLOT[c], [P, CHUNKS[c], PACK], BF16)
+            interleave(nc.scalar.copy, grouped[c][:], products[c][:])
+
+        def quant(c):
+            quantized[c] = quantize(grouped[c], CHUNKS[c], CODES_SLOT[c])
+
+        def pieces_of(c):
+            n = min(CHUNKS[c], C)
+            return [((starts[c] + a) // C, n) for a in range(0, CHUNKS[c], n)]
+
+        def mult(c, tiles=(0, 1)):
             width = CHUNKS[c]
-            grouped = ring.tile([P, width, PACK], BF16, name="grouped", tag="grouped", align_bytes=64)
-            interleave(grouped[:], g[:])
-            codes, scales = quantize(grouped, width)
-            n = min(width, C)
-            pieces = [((starts[c] + a) // C, n) for a in range(0, width, n)]
-            multiply(codes, scales, pieces, [d[:, starts[c] : starts[c] + width] for d in dx])
+            for m in tiles:
+                bank = mx_bank()
+                multiply(bank[:, :width], m, *quantized[c], pieces_of(c))
+                nc.scalar.copy(out=dx[m][:, starts[c] : starts[c] + width], in_=bank[:, :width])
 
-        products = [product_tile(c) for c in range(HEAD)]
-        for j in range(PACK):
-            for c in range(HEAD):
-                gather_plane(c, products[c], j)
-        for c in range(len(CHUNKS)):
-            ahead = c + 1
-            if HEAD <= ahead < len(CHUNKS):
-                products.append(product_tile(ahead))
-                for j in range(PACK):
-                    gather_plane(ahead, products[ahead], j)
-            finish_chunk(c, products[c])
+        gather([0, 1])
+        group(0)
+        group(1)
+        gather([2])
+        quant(0)
+        quant(1)
+        mult(0)
+        group(2)
+        mult(1)
+        for c in range(2, 6):
+            gather([c + 1])
+            quant(c)
+            group(c + 1)
+            mult(c)
+        gather([7])
+        gather([8])
+        quant(6)
+        group(7)
+        group(8)
+        mult(6, [0])
+        gather([9])
+        quant(7)
+        group(9)
+        quant(8)
+        mult(7, [0])
+        quant(9)
+        mult(8, [0])
+        mult(9, [0])
+        mult(6, [1])
+        bank = psum.tile([P, BANK], F32, name="sum_bank", tag="sum_bank")
+        for c in (7, 8, 9):
+            at = starts[c] - starts[7]
+            multiply(bank[:, at : at + CHUNKS[c]], 1, *quantized[c], pieces_of(c))
+        nc.scalar.copy(out=dx[1][:, starts[7] :], in_=bank[:])
 
-        for h in range(T // BANK):
-            grouped = keep.tile([P, BANK, PACK], BF16, name=f"shared{h}", align_bytes=64)
-            for a in range(0, BANK, SHARED_PIECE):
-                interleave(grouped[:, a : a + SHARED_PIECE, :], dy_again[h][:, :, a : a + SHARED_PIECE])
-            codes, scales = quantize(grouped, BANK)
-            multiply(codes, scales, [(E, BANK)], [d[:, h * BANK : (h + 1) * BANK] for d in ds])
+        shared0 = slot_tile("gate9b", [P, BANK, PACK], BF16)
+        for a in range(0, BANK, SHARED_PIECE):
+            interleave(nc.vector.tensor_copy, shared0[:, a : a + SHARED_PIECE, :], rounded[:, :, a : a + SHARED_PIECE])
+        shared = [quantize(shared0, BANK), quantize(shared1, BANK, "gate9a")]
+        for m in range(K // P):
+            for h in range(T // BANK):
+                bank = mx_bank()
+                multiply(bank[:], m, *shared[h], [(E, BANK)])
+                nc.scalar.copy(out=ds[m][:, h * BANK : (h + 1) * BANK], in_=bank[:])
 
         def fetch(m, h, r):
-            got = ring.tile([P, BANK], F32, name="got", tag="got", bufs=8)
+            got = ring.tile([P, BANK], F32, name="got", tag="got", bufs=10)
             cols = slice(h * BANK // STRIPE, (h + 1) * BANK // STRIPE)
             nc.vector.tensor_copy(got[:], dx[m][:].indirect(pos_sb[r][:, cols]))
             return got
@@ -186,9 +242,10 @@ def tile_moe_bds_lin_none_kernel(
 
         def sum_terms(m, h, count):
             bank = psum.tile([P, BANK], F32, name="sum_bank", tag="sum_bank")
-            add_turned(bank, ds[m][:, h * BANK : (h + 1) * BANK], True, False)
             for r in range(count):
-                add_turned(bank, fetch(m, h, r), False, r == count - 1)
+                add_turned(bank, fetch(m, h, r), r == 0, r == count - 1)
+                if r == 0:
+                    add_turned(bank, ds[m][:, h * BANK : (h + 1) * BANK], False, False)
             turned = ring.tile([P, BANK], F32, name="turned", tag="turned")
             nc.scalar.copy(out=turned[:], in_=bank[:])
             back = psum.tile([P, BANK], F32, name="back_bank", tag="back_bank")

@@ -25,10 +25,12 @@ BANK = 512
 STRIPE = 16
 CHUNKS = [512] * 7 + [256, 128, 128]
 HEAD = 2
-GATE_SLOT = ["gate0", "gate1", "gate2", "gate3", "gate4", "gate0", "gate1", "gate7", "gate8"]
-PRODUCT_SLOT = ["a", "b", "c", "a", "b", "d", "a", "b", "gate7", "c"]
-GROUPED_SLOT = ["e", "a", "b", "d", "a", "b", "c", "a", "e", "b"]
-CODES_SLOT = ["gate2", "d", "gate3", "gate4", "gate0", "gate1", "gate8", None, None, None]
+PARTS = [(0, 3), (3, 4)]
+LAST_PARTS = [(0, 2), (2, 3), (3, 4)]
+GATE_SLOT = ["gate0", "gate1", "gate2", "gate3", "gate4", "gate0", "gate1", "gate7", "gate8", "gate9"]
+PRODUCT_SLOT = ["a", "b", "c", "b", "c", "b", "c", "b", "gate7_0", "c"]
+GROUPED_SLOT = ["d", "e", "d", "f", "d", "e", "d", "e", "f", "a"]
+CODES_SLOT = ["gate2_0", "f", "gate3_0", "gate4_0", "gate0_0", "gate1_0", "gate8_0", None, None, None]
 SHARED_PIECE = 128
 
 
@@ -62,15 +64,28 @@ def tile_moe_bds_lin_none_kernel(
         def slot_tile(slot, shape, dtype):
             return keep.tile(shape, dtype, name=slot, tag=slot, align_bytes=64)
 
-        def load_gate(c, slot, j0, j1, by_plane=False):
-            t = slot_tile(slot, [P, j1 - j0, CHUNKS[c]], F32)
-            src = gate_rows[:, j0:j1, starts[c] : starts[c] + CHUNKS[c]]
-            if by_plane:
-                for j in range(j1 - j0):
-                    nc.sync.dma_start(out=t[:, j, :], in_=src[:, j, :])
-            else:
-                nc.sync.dma_start(out=t[:], in_=src)
-            return [t[:, j, :] for j in range(j1 - j0)]
+        def gate_tiles(c):
+            planes = []
+            for part, (j0, j1) in enumerate(LAST_PARTS if c == last else PARTS):
+                t = slot_tile(f"{GATE_SLOT[c]}_{part}", [P, j1 - j0, CHUNKS[c]], F32)
+                planes.append((t, j0, j1))
+            return planes
+
+        def load_gate(c, parts, j0, j1):
+            for t, a, b in parts:
+                lo, hi = max(a, j0), min(b, j1)
+                if lo < hi:
+                    nc.sync.dma_start(
+                        out=t[:, lo - a : hi - a, :],
+                        in_=gate_rows[:, lo:hi, starts[c] : starts[c] + CHUNKS[c]],
+                    )
+
+        gates = {}
+
+        def open_gate(c):
+            parts = gate_tiles(c)
+            gates[c] = [t[:, j - a, :] for t, a, b in parts for j in range(a, b)]
+            return parts
 
         def load_words(e0, e1):
             nc.sync.dma_start(
@@ -79,27 +94,24 @@ def tile_moe_bds_lin_none_kernel(
             )
 
         nc.sync.dma_start(offs_sb[:], offs)
-        head = [slot_tile(GATE_SLOT[c], [P, PACK, CHUNKS[c]], F32) for c in range(HEAD)]
+        head = [open_gate(c) for c in range(HEAD + 1)]
         for j in range(PACK):
             nc.sync.dma_start(out=window[j][:], in_=dy_rows[:, j, :])
             for c in range(HEAD):
-                nc.sync.dma_start(
-                    out=head[c][:, j, :], in_=gate_rows[:, j, starts[c] : starts[c] + CHUNKS[c]]
-                )
-        gates = [[t[:, j, :] for j in range(PACK)] for t in head]
-        gates.append(load_gate(2, GATE_SLOT[2], 0, PACK, True))
-        gates.append(load_gate(3, GATE_SLOT[3], 0, PACK))
+                load_gate(c, head[c], j, j + 1)
+        for j in range(PACK):
+            load_gate(HEAD, head[HEAD], j, j + 1)
+        load_gate(3, open_gate(3), 0, PACK)
         for q in (0, 2, 1, 3):
             nc.sync.dma_start(
                 out=wscale[32 * q : 32 * q + 4, :, :].bitcast(I32),
                 in_=w_scales[:, 0, 4 * q : 4 * q + 4, :].rearrange("e f k -> f e k").bitcast(I32),
             )
         load_words(0, 6)
-        gates.append(load_gate(4, GATE_SLOT[4], 0, PACK))
+        load_gate(4, open_gate(4), 0, PACK)
         load_words(6, E + 1)
-        for c in range(5, last):
-            gates.append(load_gate(c, GATE_SLOT[c], 0, PACK))
-        gates.append(load_gate(last, "gate9a", 0, PACK - 1) + load_gate(last, "gate9b", PACK - 1, PACK))
+        for c in range(5, last + 1):
+            load_gate(c, open_gate(c), 0, PACK)
         for r, pos in enumerate((pos1, pos2, pos3, pos4)):
             nc.sync.dma_start(pos_sb[r][:], pos)
 
@@ -213,10 +225,11 @@ def tile_moe_bds_lin_none_kernel(
             multiply(bank[:, at : at + CHUNKS[c]], 1, *quantized[c], pieces_of(c))
         nc.scalar.copy(out=dx[1][:, starts[7] :], in_=bank[:])
 
-        shared0 = slot_tile("gate9b", [P, BANK, PACK], BF16)
+        shared0 = slot_tile("gate9_1", [P, BANK, PACK], BF16)
         for a in range(0, BANK, SHARED_PIECE):
             interleave(nc.vector.tensor_copy, shared0[:, a : a + SHARED_PIECE, :], rounded[:, :, a : a + SHARED_PIECE])
-        shared = [quantize(shared0, BANK), quantize(shared1, BANK, "gate9a")]
+        second = quantize(shared1, BANK, "gate9_0")
+        shared = [quantize(shared0, BANK), second]
         for m in range(K // P):
             for h in range(T // BANK):
                 bank = mx_bank()
@@ -268,6 +281,9 @@ def tile_moe_bds_lin_none_kernel(
         backs = [sum_terms(1, h, TOP - 1) for h in halves]
         lasts = [fetch(1, h, TOP - 1) for h in halves]
         for h in halves:
-            result = result_tile()
-            nc.vector.tensor_tensor(result[:], backs[h][:], lasts[h][:], ADD)
-            store(1, h, result)
+            step = BANK // (h + 1)
+            for a in range(0, BANK, step):
+                result = result_tile()
+                nc.vector.tensor_tensor(result[:, :step], backs[h][:, a : a + step], lasts[h][:, a : a + step], ADD)
+                t0 = h * BANK + a
+                nc.sync.dma_start(out=out[P:, t0 : t0 + step], in_=result[:, :step])

@@ -24,14 +24,20 @@ PACK = 4
 BANK = 512
 STRIPE = 16
 CHUNKS = [512] * 7 + [256, 128, 128]
-HEAD = 2
+HEAD = 3
+FIRST = 128
+HEAD_ORDER = (
+    [(0, 0, 0, FIRST), (0, 0, FIRST, BANK), (1, 0, 0, BANK), (2, 0, 0, BANK)]
+    + [(c, j, 0, BANK) for j in range(1, PACK) for c in (0, 1)]
+    + [(2, j, 0, BANK) for j in range(1, PACK)]
+)
 PARTS = [(0, 3), (3, 4)]
-LAST_PARTS = [(0, 2), (2, 3), (3, 4)]
 GATE_SLOT = ["gate0", "gate1", "gate2", "gate3", "gate4", "gate0", "gate1", "gate7", "gate8", "gate9"]
-PRODUCT_SLOT = ["a", "b", "c", "b", "c", "b", "c", "b", "gate7_0", "c"]
-GROUPED_SLOT = ["d", "e", "d", "f", "d", "e", "d", "e", "f", "a"]
-CODES_SLOT = ["gate2_0", "f", "gate3_0", "gate4_0", "gate0_0", "gate1_0", "gate8_0", None, None, None]
+PRODUCT_SLOT = ["a", "b", "c", "a", "c", "a", "c", "a", "gate7_0", "c"]
+GROUPED_SLOT = ["d", "e", "d", "gate2_0", "d", "e", "d", "e", "b", "f"]
+CODES_SLOT = ["gate2_0", "gate3_0", "gate3_1", "gate4_0", "gate0_0", "gate1_0", "gate8_0", None, None, None]
 SHARED_PIECE = 128
+QUARTER = 256
 
 
 def tile_moe_bds_lin_none_kernel(
@@ -66,7 +72,7 @@ def tile_moe_bds_lin_none_kernel(
 
         def gate_tiles(c):
             planes = []
-            for part, (j0, j1) in enumerate(LAST_PARTS if c == last else PARTS):
+            for part, (j0, j1) in enumerate(PARTS):
                 t = slot_tile(f"{GATE_SLOT[c]}_{part}", [P, j1 - j0, CHUNKS[c]], F32)
                 planes.append((t, j0, j1))
             return planes
@@ -94,13 +100,12 @@ def tile_moe_bds_lin_none_kernel(
             )
 
         nc.sync.dma_start(offs_sb[:], offs)
-        head = [open_gate(c) for c in range(HEAD + 1)]
-        for j in range(PACK):
-            nc.sync.dma_start(out=window[j][:], in_=dy_rows[:, j, :])
-            for c in range(HEAD):
-                load_gate(c, head[c], j, j + 1)
-        for j in range(PACK):
-            load_gate(HEAD, head[HEAD], j, j + 1)
+        for c in range(HEAD):
+            open_gate(c)
+        for c, j, a, b in HEAD_ORDER:
+            if c == 0 and a == 0:
+                nc.sync.dma_start(out=window[j][:], in_=dy_rows[:, j, :])
+            nc.sync.dma_start(out=gates[c][j][:, a:b], in_=gate_rows[:, j, starts[c] + a : starts[c] + b])
         load_gate(3, open_gate(3), 0, PACK)
         for q in (0, 2, 1, 3):
             nc.sync.dma_start(
@@ -121,10 +126,10 @@ def tile_moe_bds_lin_none_kernel(
             nc.scalar.copy(out=rounded[:, j, :], in_=window[j][:, :BANK])
             nc.scalar.copy(out=shared1[:, :, j], in_=window[j][:, BANK:])
 
-        def gather_plane(c, g, j):
-            cols = slice(starts[c] // STRIPE, (starts[c] + CHUNKS[c]) // STRIPE)
+        def gather_plane(c, j, a, b):
+            cols = slice((starts[c] + a) // STRIPE, (starts[c] + b) // STRIPE)
             nc.vector.tensor_tensor(
-                g[:, j, :], window[j][:].indirect(offs_sb[:, cols]), gates[c][j], MULT
+                products[c][:, j, a:b], window[j][:].indirect(offs_sb[:, cols]), gates[c][j][:, a:b], MULT
             )
 
         def interleave(copy, dst, src):
@@ -165,12 +170,13 @@ def tile_moe_bds_lin_none_kernel(
 
         products, grouped, quantized = {}, {}, {}
 
-        def gather(chunks):
-            for c in chunks:
-                products[c] = slot_tile(PRODUCT_SLOT[c], [P, PACK, CHUNKS[c]], F32)
+        def open_product(c):
+            products[c] = slot_tile(PRODUCT_SLOT[c], [P, PACK, CHUNKS[c]], F32)
+
+        def gather(c):
+            open_product(c)
             for j in range(PACK):
-                for c in chunks:
-                    gather_plane(c, products[c], j)
+                gather_plane(c, j, 0, CHUNKS[c])
 
         def group(c):
             grouped[c] = slot_tile(GROUPED_SLOT[c], [P, CHUNKS[c], PACK], BF16)
@@ -190,27 +196,42 @@ def tile_moe_bds_lin_none_kernel(
                 multiply(bank[:, :width], m, *quantized[c], pieces_of(c))
                 nc.scalar.copy(out=dx[m][:, starts[c] : starts[c] + width], in_=bank[:, :width])
 
-        gather([0, 1])
+        for c in range(HEAD):
+            open_product(c)
+        for step in HEAD_ORDER:
+            gather_plane(*step)
         group(0)
         group(1)
-        gather([2])
         quant(0)
-        quant(1)
-        mult(0)
         group(2)
+        mult(0)
+        gather(3)
+        quant(1)
+        quant(2)
+        group(3)
         mult(1)
-        for c in range(2, 6):
-            gather([c + 1])
-            quant(c)
-            group(c + 1)
-            mult(c)
-        gather([7])
-        gather([8])
+        mult(2)
+        gather(4)
+        quant(3)
+        group(4)
+        mult(3)
+        middle = slot_tile("gate4_0", [P, QUARTER, PACK], BF16)
+        interleave(nc.scalar.copy, middle[:], rounded[:, :, QUARTER:])
+        gather(5)
+        quant(4)
+        group(5)
+        mult(4)
+        gather(6)
+        quant(5)
+        group(6)
+        mult(5, [0])
+        gather(7)
+        gather(8)
         quant(6)
         group(7)
         group(8)
         mult(6, [0])
-        gather([9])
+        gather(9)
         quant(7)
         group(9)
         quant(8)
@@ -219,22 +240,32 @@ def tile_moe_bds_lin_none_kernel(
         mult(8, [0])
         mult(9, [0])
         mult(6, [1])
-        bank = psum.tile([P, BANK], F32, name="sum_bank", tag="sum_bank")
-        for c in (7, 8, 9):
-            at = starts[c] - starts[7]
-            multiply(bank[:, at : at + CHUNKS[c]], 1, *quantized[c], pieces_of(c))
-        nc.scalar.copy(out=dx[1][:, starts[7] :], in_=bank[:])
+        for tag, chunks in (("back_bank", (5,)), ("sum_bank", (7, 8, 9))):
+            bank = psum.tile([P, BANK], F32, name=tag, tag=tag)
+            s0 = starts[chunks[0]]
+            for c in chunks:
+                at = starts[c] - s0
+                multiply(bank[:, at : at + CHUNKS[c]], 1, *quantized[c], pieces_of(c))
+            nc.scalar.copy(out=dx[1][:, s0 : s0 + BANK], in_=bank[:])
 
-        shared0 = slot_tile("gate9_1", [P, BANK, PACK], BF16)
-        for a in range(0, BANK, SHARED_PIECE):
+        shared0 = slot_tile("gate9_0", [P, QUARTER, PACK], BF16)
+        for a in range(0, QUARTER, SHARED_PIECE):
             interleave(nc.vector.tensor_copy, shared0[:, a : a + SHARED_PIECE, :], rounded[:, :, a : a + SHARED_PIECE])
-        second = quantize(shared1, BANK, "gate9_0")
-        shared = [quantize(shared0, BANK), second]
+        codes = [slot_tile(GROUPED_SLOT[last - 1 + h], [P, BANK], U32) for h in range(2)]
+        scales = keep.tile([P, T], U8, name="shared_scales", align_bytes=64)
+        for src, t0, t1 in ((middle, QUARTER, BANK), (shared0, 0, QUARTER), (shared1, BANK, T)):
+            h = t0 // BANK
+            nc.vector.quantize_mx(
+                out=codes[h][:, t0 - h * BANK : t1 - h * BANK].bitcast(FP8X4),
+                scales=scales[:, t0:t1],
+                in_=src[:].rearrange("p c j -> p (c j)"),
+            )
         for m in range(K // P):
             for h in range(T // BANK):
                 bank = mx_bank()
-                multiply(bank[:], m, *shared[h], [(E, BANK)])
-                nc.scalar.copy(out=ds[m][:, h * BANK : (h + 1) * BANK], in_=bank[:])
+                cols = slice(h * BANK, (h + 1) * BANK)
+                multiply(bank[:], m, codes[h], scales[:, cols], [(E, BANK)])
+                nc.scalar.copy(out=ds[m][:, cols], in_=bank[:])
 
         def fetch(m, h, r):
             got = ring.tile([P, BANK], F32, name="got", tag="got", bufs=10)

@@ -64,7 +64,7 @@ def tile_moe_bds_lin_none_kernel(
         ds = [keep.tile([P, T], F32, name=f"ds{m}") for m in range(K // P)]
         ident = keep.tile([P, P], F32, name="ident")
 
-        nc.gpsimd.memset(wscale[:].rearrange("p e k -> p (e k)").bitcast(I32), 0)
+        nc.vector.memset(wscale[:].rearrange("p e k -> p (e k)").bitcast(I32), 0)
         make_identity(nc, ident[:])
 
         def slot_tile(slot, shape, dtype):
@@ -112,10 +112,9 @@ def tile_moe_bds_lin_none_kernel(
                 out=wscale[32 * q : 32 * q + 4, :, :].bitcast(I32),
                 in_=w_scales[:, 0, 4 * q : 4 * q + 4, :].rearrange("e f k -> f e k").bitcast(I32),
             )
-        load_words(0, 6)
-        load_gate(4, open_gate(4), 0, PACK)
-        load_words(6, E + 1)
-        for c in range(5, last + 1):
+        for c in range(4, last + 1):
+            if c < 8:
+                load_words(4 * (c - 4), 4 * (c - 3) + (c == 7))
             load_gate(c, open_gate(c), 0, PACK)
         for r, pos in enumerate((pos1, pos2, pos3, pos4)):
             nc.sync.dma_start(pos_sb[r][:], pos)

from contextlib import ExitStack

import concourse.mybir as mybir
from concourse.masks import make_identity

K, T, E, C, N = 256, 1024, 16, 256, 512
TOP = 4
S = E * C
FLOPS = 2 * N * K * (S + T)

F32 = mybir.dt.float32
BF16 = mybir.dt.bfloat16
I32 = mybir.dt.int32
U32 = mybir.dt.uint32
U16 = mybir.dt.uint16
U8 = mybir.dt.uint8
FP8X4 = mybir.dt.float8_e4m3fn_x4
FP4X4 = mybir.dt.float4_e2m1fn_x4
MULT = mybir.AluOpType.mult
ADD = mybir.AluOpType.add

P = 128
PACK = 4
BANK = 512
STRIPE = 16
CHUNKS = [512] * 7 + [256, 128, 128]
HEAD = 3
FIRST = 128
HEAD_ORDER = (
    [(0, 0, 0, FIRST), (0, 0, FIRST, BANK), (1, 0, 0, BANK), (2, 0, 0, BANK)]
    + [(c, j, 0, BANK) for j in range(1, PACK) for c in (0, 1)]
    + [(2, j, 0, BANK) for j in range(1, PACK)]
)
PARTS = [(0, 3), (3, 4)]
GATE_SLOT = ["gate0", "gate1", "gate2", "gate3", "gate4", "gate0", "gate1", "gate7", "gate8", "gate9"]
PRODUCT_SLOT = ["a", "b", "c", "a", "c", "a", "c", "a", "gate7_0", "c"]
GROUPED_SLOT = ["d", "e", "d", "gate2_0", "d", "e", "d", "e", "b", "f"]
CODES_SLOT = ["gate2_0", "gate3_0", "gate3_1", "gate4_0", "gate0_0", "gate1_0", "gate8_0", None, None, None]
SHARED_PIECE = 128
QUARTER = 256


def tile_moe_bds_lin_none_kernel(
    tc, dyT, w_words, w_scales, gate, offs, pos1, pos2, pos3, pos4, out
):
    nc = tc.nc
    starts = [sum(CHUNKS[:c]) for c in range(len(CHUNKS))]
    last = len(CHUNKS) - 1
    dy_rows = dyT.rearrange("(p j) t -> p j t", j=PACK)
    gate_rows = gate.rearrange("(p j) s -> p j s", j=PACK)

    with ExitStack() as ctx:
        lists = ctx.enter_context(tc.tile_pool(name="lists", bufs=1))
        keep = ctx.enter_context(tc.tile_pool(name="keep", bufs=1))
        ring = ctx.enter_context(tc.tile_pool(name="ring", bufs=3))
        psum = ctx.enter_context(tc.psum_pool(name="psum", bufs=2))

        offs_sb = lists.tile([P, S // STRIPE], U16, name="offs_sb")
        pos_sb = [lists.tile([P, T // STRIPE], U16, name=f"pos_sb{r}") for r in range(TOP)]
        window = [keep.tile([P, T], F32, name=f"window{j}") for j in range(PACK)]
        words = keep.tile([P, E + 1, 2 * K], U8, name="words", align_bytes=64)
        wscale = keep.tile([P, E + 1, K], U8, name="wscale", align_bytes=64)
        dx = [keep.tile([P, S], F32, name=f"dx{m}") for m in range(K // P)]
        ds = [keep.tile([P, T], F32, name=f"ds{m}") for m in range(K // P)]
        ident = keep.tile([P, P], F32, name="ident")

        nc.vector.memset(wscale[:].rearrange("p e k -> p (e k)").bitcast(I32), 0)
        make_identity(nc, ident[:])

        def slot_tile(slot, shape, dtype):
            return keep.tile(shape, dtype, name=slot, tag=slot, align_bytes=64)

        def gate_tiles(c):
            planes = []
            for part, (j0, j1) in enumerate(PARTS):
                t = slot_tile(f"{GATE_SLOT[c]}_{part}", [P, j1 - j0, CHUNKS[c]], F32)
                planes.append((t, j0, j1))
            return planes

        def load_gate(c, parts, j0, j1):
            for t, a, b in parts:
                lo, hi = max(a, j0), min(b, j1)
                if lo < hi:
                    nc.sync.dma_start(
                        out=t[:, lo - a : hi - a, :],
                        in_=gate_rows[:, lo:hi, starts[c] : starts[c] + CHUNKS[c]],
                    )

        gates = {}

        def open_gate(c):
            parts = gate_tiles(c)
            gates[c] = [t[:, j - a, :] for t, a, b in parts for j in range(a, b)]
            return parts

        def load_words(e0, e1):
            nc.sync.dma_start(
                out=words[:, e0:e1, :].bitcast(I32),
                in_=w_words[e0:e1, 0].rearrange("e p b -> p e b").bitcast(I32),
            )

        nc.sync.dma_start(offs_sb[:], offs)
        for c in range(HEAD):
            open_gate(c)
        for c, j, a, b in HEAD_ORDER:
            if c == 0 and a == 0:
                nc.sync.dma_start(out=window[j][:], in_=dy_rows[:, j, :])
            nc.sync.dma_start(out=gates[c][j][:, a:b], in_=gate_rows[:, j, starts[c] + a : starts[c] + b])
        load_gate(3, open_gate(3), 0, PACK)
        for q in (0, 2, 1, 3):
            nc.sync.dma_start(
                out=wscale[32 * q : 32 * q + 4, :, :].bitcast(I32),
                in_=w_scales[:, 0, 4 * q : 4 * q + 4, :].rearrange("e f k -> f e k").bitcast(I32),
            )
        for c in range(4, last + 1):
            if c < 8:
                load_words(4 * (c - 4), 4 * (c - 3) + (c == 7))
            load_gate(c, open_gate(c), 0, PACK)
        for r, pos in enumerate((pos1, pos2, pos3, pos4)):
            nc.sync.dma_start(pos_sb[r][:], pos)

        rounded = keep.tile([P, PACK, BANK], BF16, name="rounded")
        shared1 = keep.tile([P, BANK, PACK], BF16, name="shared1", align_bytes=64)
        for j in range(PACK):
            nc.scalar.copy(out=rounded[:, j, :], in_=window[j][:, :BANK])
            nc.scalar.copy(out=shared1[:, :, j], in_=window[j][:, BANK:])

        def gather_plane(c, j, a, b):
            cols = slice((starts[c] + a) // STRIPE, (starts[c] + b) // STRIPE)
            nc.vector.tensor_tensor(
                products[c][:, j, a:b], window[j][:].indirect(offs_sb[:, cols]), gates[c][j][:, a:b], MULT
            )

        def interleave(copy, dst, src):
            copy(
                out=dst.rearrange("p (c i) j -> p c j i", i=4),
                in_=src.rearrange("p j (c i) -> p c j i", i=4),
            )

        def quantize(grouped, width, slot=None):
            if slot:
                codes = slot_tile(slot, [P, width], U32)
            else:
                codes = ring.tile([P, width], U32, name="codes", tag="codes", bufs=4, align_bytes=64)
            scales = ring.tile([P, width], U8, name="scales", tag="scales", bufs=7, align_bytes=64)
            nc.vector.quantize_mx(
                out=codes[:].bitcast(FP8X4),
                scales=scales[:],
                in_=grouped[:].rearrange("p c j -> p (c j)"),
            )
            return codes, scales

        def mx_bank():
            return psum.tile([P, BANK], F32, name="mx_bank", tag="mx_bank", bufs=4)

        def multiply(bank, m, codes, scales, pieces):
            at = 0
            for e, n in pieces:
                nc.tensor.matmul_mx(
                    out=bank[:, at : at + n],
                    lhsT=words[:, e, 2 * P * m : 2 * P * (m + 1)].bitcast(FP4X4),
                    lhsT_scale=wscale[:, e, P * m : P * (m + 1)],
                    rhs=codes[:, at : at + n].bitcast(FP8X4),
                    rhs_scale=scales[:, at : at + n],
                    start=True,
                    stop=True,
                )
                at += n

        products, grouped, quantized = {}, {}, {}

        def open_product(c):
            products[c] = slot_tile(PRODUCT_SLOT[c], [P, PACK, CHUNKS[c]], F32)

        def gather(c):
            open_product(c)
            for j in range(PACK):
                gather_plane(c, j, 0, CHUNKS[c])

        def group(c):
            grouped[c] = slot_tile(GROUPED_SLOT[c], [P, CHUNKS[c], PACK], BF16)
            interleave(nc.scalar.copy, grouped[c][:], products[c][:])

        def quant(c):
            quantized[c] = quantize(grouped[c], CHUNKS[c], CODES_SLOT[c])

        def pieces_of(c):
            n = min(CHUNKS[c], C)
            return [((starts[c] + a) // C, n) for a in range(0, CHUNKS[c], n)]

        def mult(c, tiles=(0, 1)):
            width = CHUNKS[c]
            for m in tiles:
                bank = mx_bank()
                multiply(bank[:, :width], m, *quantized[c], pieces_of(c))
                nc.scalar.copy(out=dx[m][:, starts[c] : starts[c] + width], in_=bank[:, :width])

        for c in range(HEAD):
            open_product(c)
        for step in HEAD_ORDER:
            gather_plane(*step)
        group(0)
        group(1)
        quant(0)
        group(2)
        mult(0)
        gather(3)
        quant(1)
        quant(2)
        group(3)
        mult(1)
        mult(2)
        gather(4)
        quant(3)
        group(4)
        mult(3)
        middle = slot_tile("gate4_0", [P, QUARTER, PACK], BF16)
        interleave(nc.scalar.copy, middle[:], rounded[:, :, QUARTER:])
        gather(5)
        quant(4)
        group(5)
        mult(4)
        gather(6)
        quant(5)
        group(6)
        mult(5, [0])
        gather(7)
        gather(8)
        quant(6)
        group(7)
        group(8)
        mult(6, [0])
        gather(9)
        quant(7)
        group(9)
        quant(8)
        mult(7, [0])
        quant(9)
        mult(8, [0])
        mult(9, [0])
        mult(6, [1])
        for tag, chunks in (("back_bank", (5,)), ("sum_bank", (7, 8, 9))):
            bank = psum.tile([P, BANK], F32, name=tag, tag=tag)
            s0 = starts[chunks[0]]
            for c in chunks:
                at = starts[c] - s0
                multiply(bank[:, at : at + CHUNKS[c]], 1, *quantized[c], pieces_of(c))
            nc.scalar.copy(out=dx[1][:, s0 : s0 + BANK], in_=bank[:])

        shared0 = slot_tile("gate9_0", [P, QUARTER, PACK], BF16)
        for a in range(0, QUARTER, SHARED_PIECE):
            interleave(nc.vector.tensor_copy, shared0[:, a : a + SHARED_PIECE, :], rounded[:, :, a : a + SHARED_PIECE])
        codes = [slot_tile(GROUPED_SLOT[last - 1 + h], [P, BANK], U32) for h in range(2)]
        scales = keep.tile([P, T], U8, name="shared_scales", align_bytes=64)
        for src, t0, t1 in ((middle, QUARTER, BANK), (shared0, 0, QUARTER), (shared1, BANK, T)):
            h = t0 // BANK
            nc.vector.quantize_mx(
                out=codes[h][:, t0 - h * BANK : t1 - h * BANK].bitcast(FP8X4),
                scales=scales[:, t0:t1],
                in_=src[:].rearrange("p c j -> p (c j)"),
            )
        for m in range(K // P):
            for h in range(T // BANK):
                bank = mx_bank()
                cols = slice(h * BANK, (h + 1) * BANK)
                multiply(bank[:], m, codes[h], scales[:, cols], [(E, BANK)])
                nc.scalar.copy(out=ds[m][:, cols], in_=bank[:])

        def fetch(m, h, r):
            got = ring.tile([P, BANK], F32, name="got", tag="got", bufs=10)
            cols = slice(h * BANK // STRIPE, (h + 1) * BANK // STRIPE)
            nc.vector.tensor_copy(got[:], dx[m][:].indirect(pos_sb[r][:, cols]))
            return got

        def add_turned(bank, term, first, last):
            for b in range(BANK // P):
                nc.tensor.matmul(
                    bank[:, b * P : (b + 1) * P],
                    term[:, b * P : (b + 1) * P],
                    ident[:],
                    start=first and b == 0,
                    stop=last and b == BANK // P - 1,
                    is_transpose=True,
                )

        def sum_terms(m, h, count):
            bank = psum.tile([P, BANK], F32, name="sum_bank", tag="sum_bank")
            for r in range(count):
                add_turned(bank, fetch(m, h, r), r == 0, r == count - 1)
                if r == 0:
                    add_turned(bank, ds[m][:, h * BANK : (h + 1) * BANK], False, False)
            turned = ring.tile([P, BANK], F32, name="turned", tag="turned")
            nc.scalar.copy(out=turned[:], in_=bank[:])
            back = psum.tile([P, BANK], F32, name="back_bank", tag="back_bank")
            for b in range(BANK // P):
                nc.tensor.transpose(back[:, b * P : (b + 1) * P], turned[:, b * P : (b + 1) * P], ident[:])
            return back

        def store(m, h, result):
            nc.sync.dma_start(out=out[m * P : (m + 1) * P, h * BANK : (h + 1) * BANK], in_=result[:])

        def result_tile():
            return ring.tile([P, BANK], F32, name="result", tag="result", bufs=4)

        halves = range(T // BANK)
        for h in halves:
            back = sum_terms(0, h, TOP)
            result = result_tile()
            nc.scalar.copy(out=result[:], in_=back[:])
            store(0, h, result)
        backs = [sum_terms(1, h, TOP - 1) for h in halves]
        lasts = [fetch(1, h, TOP - 1) for h in halves]
        for h in halves:
            step = BANK // (h + 1)
            for a in range(0, BANK, step):
                result = result_tile()
                nc.vector.tensor_tensor(result[:, :step], backs[h][:, a : a + step], lasts[h][:, a : a + step], ADD)
                t0 = h * BANK + a
                nc.sync.dma_start(out=out[P:, t0 : t0 + step], in_=result[:, :step])
